import numpy as np, ml_dtypes
CORES = [40,64,80,88,96,104,120,144]
N = 8
BF = ml_dtypes.bfloat16
C, P, WA, WM, MC, RO = 64, 16, 2048, 2048, 32, 3
L0, LM, AM, Q, B = 3, 7, 3, 2048 // 64, 32 // 16
def block(rng, n):
    q = rng.integers(24, 257, (N, 8, 16, n // P, 1))
    return (rng.random((N, 8, 16, n // P, P)) * q).astype(np.int64).reshape(N, 8, 16, n)
def parts(rng):
    X = block(rng, C * P); A = block(rng, WA); M = rng.integers(0, 256, (N, 8, 16, WM))
    w = rng.integers(0, 256, (N, 8, 16, 2)); k = rng.integers(0, 2048, (N, 8, 2, MC))
    t = np.stack([rng.integers(700, 1101, (N, 8)), rng.integers(700, 1001, (N, 8))], axis=2)
    return X, A, M, w, k, t
def pack(X, A, M, w, k, t):
    b = lambda v: np.ascontiguousarray(v.reshape(N, 128, -1)).astype(np.float32).astype(BF)
    h = k.reshape(N, 8, 2, B, 16).transpose(0, 1, 4, 2, 3).reshape(N, 128, 2 * B)
    return {"gn": b(X), "ar": b(A), "mh": b(M), "wt": b(w), "hk": np.ascontiguousarray(h).astype(np.int32), "th": np.repeat(t, 16, axis=1).astype(np.int32)}
def setup_inputs(rng):
    return pack(*parts(rng))
def setup_inputs_ties(rng):
    X, A, M, w, k, t = parts(rng)
    return pack((X >> 4) << 4, (A >> 4) << 4, (M >> 4) << 4, w | 1, k, (t >> 4) << 4)
def setup_inputs_ends(rng):
    X, A, M, w, k, t = parts(rng); E = X.reshape(N, 8, 16, C, P); c = np.arange(C); uu = np.arange(4096)
    k[:, 1::2, :, 0] = 0; k[:, 1::2, :, MC - 1] = 2047
    for q in range(N):
        for g in range(0, 8, 2):
            o = (2 * rng.permutation(2048)[:64] + 1) | (LM << 4)
            s = ((o * o >> 5)[:, None] + o[:, None] * np.arange(2048)[None, :]) & (WA - 1)
            j = int(np.argmax(s)); key = j % 2048; k[q, g, 0] = key
            near = np.argsort(((uu * uu >> 5) + key * uu) & (WA - 1))[-64:]
            u = near[rng.integers(0, 64, C)]; u[0] = 0; u[1] = o[j // 2048]; u[C - 1] = o[j // 2048]
            w[q, g, :, 0] = 0; w[q, g, 0, 0] = 1; w[q, g, 1, 0] = 128
            E[q, g, 0, c, c & AM] = u & 127; E[q, g, 1, c, c & AM] = u >> 7
    t[:, ::2, 0] = 4096; t[:, 0, 1] = 0
    return pack(E.reshape(N, 8, 16, C * P), A, M, w, k, t)
def setup_inputs_edges(rng):
    X, A, M, w, k, t = parts(rng)
    t[:, 0, 0] = 0; t[:, 1, 1] = 4096; t[:, 2, 0] = 4096; t[:, 2, 1] = 0; t[:, 3] = 1
    pat = rng.integers(0, 256, (16, 2)); pat[0, 0] = 3; pat[0, 1] = 200
    X[:, 3] = np.where(rng.random((N, 1, C * P)) < 0.5, pat[None, :, :1], pat[None, :, 1:])
    A[:, 3] = np.where(rng.random((N, 1, WA)) < 0.5, pat[None, :, :1], pat[None, :, 1:])
    M[:, 3] = np.where(rng.random((N, 1, WM)) < 0.06, np.max(pat, axis=1)[None, :, None], M[:, 3])
    w[:, 4] = rng.integers(240, 256, (N, 16, 2))
    X[:, 4] = rng.integers(200, 256, (N, 16, C * P)); A[:, 4] = rng.integers(200, 256, (N, 16, WA)); M[:, 4] = rng.integers(200, 256, (N, 16, WM))
    t[:, 4, 0] = rng.integers(230, 331, N); t[:, 4, 1] = rng.integers(230, 301, N)
    for g, lo in ((5, 150), (7, 70)):
        lev = int(rng.integers(lo, 241))
        X[:, g] = rng.integers(0, 16, (N, 16, C * P)) + (lev if g == 7 else 0)
        A[:, g] = rng.integers(0, 16, (N, 16, WA)) + (lev if g == 5 else 0)
        M[:, g] = rng.integers(0, 16, (N, 16, WM))
        t[:, g, 0] = 16 * lev + 4 * rng.integers(-5, 6, N) + rng.integers(0, 2, N)
        t[:, g, 1] = 16 * lev + 4 * rng.integers(10, 19, N) + rng.integers(0, 2, N)
    pa = rng.integers(0, 256, (16, 8))
    jx = np.repeat(rng.integers(0, 8, (N, C)), P, axis=1); ja = np.repeat(rng.integers(0, 8, (N, WA // P)), P, axis=1)
    jx = np.where((np.arange(C * P) // P) % 8 < 4, jx, rng.integers(0, 8, (N, C * P)))
    X[:, 6] = pa[:, jx].transpose(1, 0, 2); A[:, 6] = pa[:, ja].transpose(1, 0, 2)
    t[:, 6, 0] = 1; t[:, 6, 1] = 0
    return pack(X, A, M, w, k, t)
def setup_inputs_alike(rng):
    X, A, M, w, k, t = parts(rng); E = X.reshape(N, 8, 16, C, P); H = A.reshape(N, 8, 16, WA // P, P)
    E[:, ::2] = np.repeat(E[:, ::2, :, :1], C, axis=3); E[:, :, :, 5::8] = 0
    H[:, 1::2] = np.tile(H[:, 1::2, :, :4], (1, 1, 1, WA // P // 4, 1))
    M[:, 3::4] = M[:, 3::4][..., rng.integers(0, 8, WM)]
    k[..., 1::2] = k[..., ::2]
    return pack(E.reshape(N, 8, 16, C * P), H.reshape(N, 8, 16, WA), M, w, k, t)
def setup_inputs_spread(rng):
    X, A, M, w, k, t = parts(rng)
    X = (np.exp2(8 * rng.random((N, 8, 1, C * P))) * rng.random(X.shape)).astype(np.int64)
    A = (np.exp2(8 * rng.random((N, 8, 1, WA))) * rng.random(A.shape)).astype(np.int64)
    M = (np.exp2(4 + 4 * rng.random((N, 8, 1, WM))) * (0.5 + 0.5 * rng.random(M.shape))).astype(np.int64)
    w = np.exp2(8 * rng.random(w.shape)).astype(np.int64); k = np.exp2(11 * rng.random(k.shape)).astype(np.int64)
    t = np.stack([np.exp2(6.5 + 3.5 * rng.random((N, 8))), np.exp2(9 + 2 * rng.random((N, 8)))], axis=2).astype(np.int64)
    return pack(np.minimum(X, 255), np.minimum(A, 255), np.minimum(M, 255), np.minimum(w, 255), np.minimum(k, 2047), t)
def check_inputs(d):
    bad = []
    for s in ("gn", "ar", "mh", "wt"):
        v = d[s].astype(np.float32)
        if not (np.all(v >= 0) and np.all(v <= 255) and np.all(v == np.floor(v))): bad.append("whole numbers from 0 to 255 in " + s)
    for s, hi in (("hk", 2047), ("th", 4096)):
        if np.min(d[s]) < 0 or np.max(d[s]) > hi: bad.append("range of " + s)
    v = d["th"].reshape(N, 8, 16, 2)
    if not np.all(v == v[:, :, :1]): bad.append("th alike in the rows of a group")
    return bad
def pick(a, ix):
    return np.take_along_axis(a, ix.reshape(N, 8, 1, -1), 3).reshape((N, 8, 16) + ix.shape[2:])
def reference(gn, ar, mh, wt, hk, th):
    ints = lambda v: v.astype(np.float32).astype(np.int64)
    X = ints(gn).reshape(N, 8, 16, C, P); A = ints(ar).reshape(N, 8, 16, WA); M = ints(mh).reshape(N, 8, 16, WM); w = ints(wt).reshape(N, 8, 16, 2)
    k = hk.astype(np.int64).reshape(N, 8, 16, 2, B).transpose(0, 1, 3, 4, 2).reshape(N, 8, 2, MC)
    lim = th.astype(np.int64).reshape(N, 8, 16, 2)[:, :, 0, :, None, None]
    c = np.arange(C); m = np.arange(MC); i = np.arange(P)
    for t in range(RO):
        d = 1 + t % (N - 1); a = (c + 3 * t) & AM
        xa = X[:, :, :, c, a]
        u = np.add.reduce(w[..., 0:1] * xa, axis=2) & 4095
        p = ((u * u >> 5)[..., None] + k[:, :, 0, None, :] * u[..., None]) & (WA - 1)
        l = L0 + ((u[..., None] * (2 * m + 1) >> 4) & LM)
        d1 = np.add.reduce(np.abs(pick(A, p) - xa[..., None]), axis=2)
        xe = pick(X.reshape(N, 8, 16, C * P), (P * c + a)[:, None] + l)
        d2 = np.add.reduce(np.abs(pick(A, (p + l) & (WA - 1)) - xe), axis=2)
        score = np.where((d1 < lim[:, :, 0]) & (d2 < lim[:, :, 0]), l * MC + (MC - 1 - m), -1)
        best = np.argmax(score, axis=3)[..., None]
        lb = np.where(np.max(score, axis=3)[..., None] >= 0, np.take_along_axis(l, best, 3), 0); pb = np.take_along_axis(p, best, 3)
        inside = (i > a[:, None]) & (i < a[:, None] + lb)
        trial = np.where(inside[:, :, None], pick(A, (pb + i - a[:, None]) & (WA - 1)), X)
        z = np.roll(np.max(trial, axis=4), d, axis=0)
        v = np.add.reduce(w[..., 1:2] * z, axis=2) & 4095
        pm = ((v * v >> 5)[..., None] + k[:, :, 1, None, :] * v[..., None]) & (WM - 1)
        dm = np.add.reduce(np.abs(pick(M, pm) - z[..., None]), axis=2)
        known = np.any(dm < lim[:, :, 1], axis=3)
        np.put_along_axis(M, (C * (v & (Q - 1)) + c)[:, :, None, :], z, 3)
        new = np.roll(np.logical_not(known), -d, axis=0)
        X = np.where(new[:, :, None, :, None], trial, X)
        over = new & ((c & 3) == (t & 3))
        head = np.where(over[:, :, None, :, None], trial, A[..., :C * P].reshape(N, 8, 16, C, P))
        A = np.concatenate([head.reshape(N, 8, 16, C * P), A[..., C * P:]], axis=3)
    return {"y": np.ascontiguousarray(X).reshape(N, 128, C * P).astype(np.float32).astype(BF)}

from concourse.bass import DstId, RemoteDMATransfer
from concourse.mybir import AluOpType as Op, AxisListType, ActivationFunctionType as Fn

A0 = 4128
XO = 2080
TC = (3104, 4128, 5152)
BIG = float(2 ** 21)
G1PE = (0, 0, 0, 0, 0, 0)
STEPS = 1500

F, I, U, B = "float32", "int32", "uint16", "bfloat16"
_COLS = {
    B: {"W": A0 + 6176, "MO": 2048, "M1": 2048, "M2": 2048, "M3": 2048, "RB": 512, "wtb": 2, "OS": 144, "WS": 432, "WB": 384, "BOs": 128,
        "RS": 256, "ON": 128, "ID": 128, "SL": 1024, "RC": 64, "RT": 64, "RA": 16, "XT": 768, "SM": 512, "XB": 3072, "XE": 2048,
        "DA": 2048, "DB": 2048, "DC": 2048, "GC": 2048, "E3": 16, "Z": 1024, "ZT": 256, "YO": 1024},
    F: {"PM": 4, "PR": 4, "PL1": 4, "PL2": 4, "PL3": 4, "ZM0": 68, "ZM1": 68, "ZR0": 68, "ZR1": 68, "ZL0": 68, "ZL1": 68, "ZL2": 68,
        "XI": 144, "G16": 128, "C": 32, "MK": 16, "BOf": 128, "J": 288, "ZE": 64, "C2K": 32, "NT": 64, "EK": 32, "KK": 64, "CB": 4,
        "TCC": 12, "UF": 40, "S0": 384, "S1": 256, "SC": 128, "E": 64, "E2": 64, "XM": 64, "RR": 8},
    I: {"hkb": 4, "thb": 2, "PI": 4, "AI": 192, "UI": 80, "Y": 256, "PP": 128, "L17": 128, "P2": 128, "LP": 384, "XX": 128, "VI": 384,
        "VC": 12, "YV": 256},
    U: {"PU": 384, "P2U": 384, "XBO": 192, "XU": 128, "TU": 64, "MU": 128, "AU": 16, "ZU": 12, "FU": 64},
}
SCRATCH = {n: ("sbuf", [128, c], d) for d, v in _COLS.items() for n, c in v.items()}
SCRATCH.update({"ps%d" % k: ("psum", [128, 512], F) for k in range(8)})
SEMAPHORES = ["dve", "act", "pe", "pool", "lx", "la", "lw", "lwt", "lhk", "lth", "lm0", "lm1", "sy0", "sy1", "sent",
              "par1", "par2", "par3", "m1", "m2", "m3", "z0", "z1", "z2", "rpar", "rq", "rz0", "rz1"]

EST = {"cyc": 1.0, "gam": 1.56, "pe": 0.55, "sem": 80.0, "sc": 3.5, "lsmall": 2300.0, "lx": 3000.0, "la": 5000.0, "lm0": 4500.0,
       "lm1": 5500.0, "par1": 5000.0, "par2": 5000.0, "par3": 5000.0, "m1": 8000.0, "m2": 14000.0, "m3": 24000.0, "zlat": 6000.0}
VARIANTS = [{}, {"cyc": 0.9, "gam": 1.15, "sem": 60.0, "sc": 2.0}, {"cyc": 1.15, "gam": 1.95, "sem": 110.0, "sc": 5.0, "pe": 0.8}]


def _build(T, sends):
    ops = []

    def add(eng, cost, r, w, fn, sem=None):
        ops.append({"eng": eng, "cost": cost, "r": r, "w": w, "fn": fn, "sem": sem})

    def ts(out, in0, s1, s2, o0, o1, r, w, n=64):
        if s2 is None:
            add(("dve",), ("v", n), r, w, lambda g, e: g.vector.tensor_scalar(out, in0, s1, None, o0))
        else:
            add(("dve",), ("v", n), r, w, lambda g, e: g.vector.tensor_scalar(out, in0, s1, s2, o0, o1))

    def tt(out, a, b, o, r, w, n=64, kind="v"):
        add(("dve",), (kind, n), r, w, lambda g, e: g.vector.tensor_tensor(out, a, b, o))

    def cp(out, a, r, w, n=64, kind="v"):
        add(("dve",), (kind, n), r, w, lambda g, e: g.vector.tensor_copy(out, a))

    def ms(out, v, w, n=64):
        add(("dve",), ("v", n), [], w, lambda g, e: g.vector.memset(out, v))

    def scan(out, a, b, init, o0, o1, r, w, n):
        add(("dve",), ("v", n), r, w, lambda g, e: g.vector.tensor_tensor_scan(out, a, b, init, o0, o1))

    def raw(out, a, r, w, n, kind="g", eng=("act", "dve")):
        add(eng, (kind, n), r, w, lambda g, e: g.vector.tensor_copy(out, a) if e == "dve" else g.scalar.activation(out, a, Fn.Copy))

    def scale(out, a, col, r, w):
        add(("act", "dve"), ("v", 64), r, w, lambda g, e: g.vector.tensor_scalar(out, a, col, None, Op.mult) if e == "dve"
            else g.scalar.activation(out, a, Fn.Copy, scale=col))

    def mag(out, a, r, w):
        add(("act",), ("v", 512), r, w, lambda g, e: g.scalar.activation(out, a, Fn.Abs))

    def mm(lst, cyc, r, w):
        def fn(g, e):
            for a in lst:
                ins = g.tensor.matmul(*a)
            return ins
        add(("pe",), ("p", cyc), r, w, fn)

    def dma(q, out, a, sem, w, r=()):
        add((q,), ("d", sem), list(r), w, lambda g, e: (g.sync if e == "sync" else g.scalar).dma_start(out, a), sem=(sem, 16))

    def ext(sem, cnt, w, r):
        add(("ext",), ("x", sem), r, w, None, sem=(sem, cnt))

    def send(r, w, key):
        add(("pool",), ("s", 0), r, ["gq"] + w, sends[key])

    def iota(out, pat, base, cm, w, n, fl):
        if fl:
            add(("pool",), ("i", n), [], w, lambda g, e: g.iota(out, pat, base, cm, allow_small_or_imprecise_dtypes=True))
        else:
            add(("pool",), ("i", n), [], w, lambda g, e: g.iota(out, pat, base, cm))

    def pick(out, a, pat, r, w, n):
        add(("pool",), ("i", n), r, w, lambda g, e: g.affine_select(out, a, pat, Op.is_equal, 0.0, 0, 1))

    W, C, XI = T.W, T.C, T.XI
    X = lambda n: XI[:, 15:15 + n]
    col = lambda t, j: t[:, j:j + 1]
    part = lambda t, a, n: t[:, a:a + n]
    ps = [T["ps%d" % k] for k in range(8)]
    cF, cG, c16, c64, c256, c4, cJ, cT = [col(C, j) for j in range(8)]
    sel = lambda t, base, f: t[:, base + 15 - f: base + 143 - f]
    cq_of = lambda h, q: 2 * q + h
    aof = lambda t, cq: (cq + 3 * t) & 3
    banks = lambda h: (ps[2 * h], ps[2 * h + 1], "b%d" % (2 * h), "b%d" % (2 * h + 1))
    xs = A0 + XO

    dma("sync", part(W, xs, 1024), T.gn[:], "lx", ["X0", "q0"])
    dma("act", T.wtb[:], T.wt[:], "lwt", ["wt", "q1"])
    dma("act", T.hkb[:], T.hk[:], "lhk", ["hk", "q1"])
    dma("act", T.thb[:], T.th[:], "lth", ["th", "q1"])
    dma("sync", T.MO[:, 0:1024], T.mh[:, 0:1024], "lm0", ["MO0", "q0"])
    dma("sync", part(W, A0, 2048), T.ar[:], "la", ["A", "q0"])
    dma("act", T.MO[:, 1024:2048], T.mh[:, 1024:2048], "lm1", ["MO1", "q1"])
    dma("act", part(W, A0 + 2048, 32), T.ar[:, 0:32], "lw", ["Aw", "q1"])
    iota(col(T.PI, 0), [[0, 1]], 0, 1, ["PI"], 1, False)
    iota(XI[:], [[1, 144]], -15, 0, ["XI"], 144, True)
    iota(T.G16[:], [[16, 8], [0, 16]], 0, 0, ["G16"], 128, True)
    iota(T.AI[:, 0:96], [[1, 2], [2, 3], [0, 16]], 0, 0, ["AI0"], 96, False)

    cp(T.PM[:, 0:2], T.hkb[:, 2:4], ["hk"], ["PM0"])
    cp(col(T.PM, 2), col(T.wtb, 1), ["wt"], ["PM1"])
    cp(col(C, 22), col(T.wtb, 0), ["wt"], ["wf"])
    ts(col(T.PM, 3), col(T.thb, 1), -BIG, None, Op.mult, None, ["th"], ["PM2"])
    send(["PM0", "PM1", "PM2"], ["sp"], "par")
    send(["MO0"], [], "m0")
    send(["MO1"], ["sm"], "m1")
    ts(col(T.PI, 1), col(T.PI, 0), 15, None, Op.bitwise_and, None, ["PI"], ["PI1"])
    ts(col(T.PI, 2), col(T.PI, 0), 112, None, Op.bitwise_and, None, ["PI"], ["PI2"])
    cp(C[:, 0:2], T.PI[:, 1:3], ["PI1", "PI2"], ["cF"])
    ts(T.WS[:, 0:144], XI[:], cG, col(C, 22), Op.is_equal, Op.mult, ["XI", "cF", "wf"], ["WS0"], 144)
    ts(T.MK[:], X(16), cF, None, Op.is_equal, None, ["XI", "cF"], ["MK"])
    ts(T.BOf[:], T.G16[:], cG, None, Op.is_equal, None, ["G16", "cF"], ["BOf"], 128)
    ts(T.BOs[:], T.G16[:], cG, BIG, Op.is_equal, Op.mult, ["G16", "cF"], ["BOs"], 128)
    ts(T.OS[:], XI[:], cG, -BIG, Op.is_equal, Op.mult, ["XI", "cF"], ["OS"], 144)
    ts(c16, cF, 16.0, float(TC[0]), Op.mult, Op.add, ["cF"], ["c16"])
    ts(c64, cF, 64.0, float(XO), Op.mult, Op.add, ["cF"], ["c64"])
    ts(c256, cF, 256.0, None, Op.mult, None, ["cF"], ["c256"])
    ts(c4, cF, 4.0, None, Op.mult, None, ["cF"], ["c4"])
    ts(cJ, cF, -131072.0, 2048.0 + 262144.0, Op.mult, Op.add, ["cF"], ["cJ"])
    ts(T.TCC[:], X(12), 256.0, c16, Op.mult, Op.add, ["XI", "c16"], ["cTc"])
    ts(C[:, 12:14], X(2), 16.0, cF, Op.mult, Op.add, ["XI", "cF"], ["cFT"])
    ts(T.CB[:, 0:2], X(2), 32.0, c64, Op.mult, Op.add, ["XI", "c64"], ["CB0"])
    ts(T.CB[:, 2:4], T.CB[:, 0:2], 16.0, None, Op.add, None, ["CB0"], ["CB1"])
    ts(C[:, 24:28], T.CB[:], c64, 1.0 / 16, Op.subtract, Op.mult, ["CB0", "CB1", "c64"], ["cq"])
    ms(T.ZE[:], 0.0, ["ZE"])
    ms(T.C2K[:], 2048.0, ["C2K"])
    ms(T.RC[:], -1.0 / 32, ["RC"])
    ms(T.RS[:], 1.0, ["RS"], 128)
    ms(T.RS[:, 0:256:16], 0.0, ["RS"])
    ms(T.ON[:], 1.0, ["ON"])
    ms(T.SL[0:32, :], -1.0, ["SL"], 512)
    pick(T.ID[:], T.ON[:], [[-1, 128]], ["ON"], ["ID"], 150)
    if any(G1PE):
        ms(T.SM[0:32, :], -1.0, ["SM"], 256)
        pick(T.SM[0:32, :], T.SM[0:32, :], [[0, 16], [-1, 32]], ["SM"], ["SM"], 530)
    pick(T.SL[0:32, :], T.SL[0:32, :], [[-1, 16], [-16, 2], [0, 32]], ["SL"], ["SL", "gq"], 1040)
    AI = T.AI[:, 96:192]
    ts(AI, T.AI[:, 0:96], 3, None, Op.bitwise_and, None, ["AI0"], ["AI"], 96)
    ts(T.J[:, 96:192], AI, 131071.0, cJ, Op.mult, Op.add, ["AI", "cJ"], ["J0"], 96)
    ts(T.J[:, 192:288], AI, cF, -BIG, Op.is_ge, Op.mult, ["AI", "cF"], ["J1"], 96)
    tt(T.J[:, 0:96], T.J[:, 96:192], T.J[:, 192:288], Op.add, ["J0", "J1"], ["J"], 192)
    ts(T.NT[:, 0:16], T.MK[:], 1.0, 1e20, Op.subtract, Op.mult, ["MK"], ["NT0"])
    ts(T.RA[:], X(16), 64.0, col(T.MK, 0), Op.mult, Op.mult, ["XI", "MK"], ["RA"])
    cp(C[:, 16:18], T.hkb[:, 0:2], ["hk"], ["hkf"])
    cp(col(C, 20), col(T.thb, 0), ["th"], ["thf"])
    for b in range(2):
        scale(part(T.EK, 16 * b, 16), T.MK[:], col(C, 16 + b), ["MK", "hkf"], ["EK%d" % b])
    mm([(ps[7][:, 0:32], T.BOf[:], T.EK[:], True, True)], 256, ["BOf", "EK0", "EK1"], ["b7"])
    cp(T.KK[:, 0:32], ps[7][:, 0:32], ["b7"], ["KK0"])
    ts(T.KK[:, 32:64], X(32), 16384.0, 8192.0, Op.mult, Op.add, ["XI"], ["KK1"])
    ts(cT, col(C, 20), c256, 0.0, Op.subtract, Op.max, ["thf", "c256"], ["cT"])
    ts(T.RT[:], T.ZE[:], cT, 256.0, Op.add, Op.min, ["ZE", "cT"], ["RT"])
    for j in (1, 2, 3):
        PL, pl = T["PL%d" % j], "PL%d" % j
        ext("par%d" % j, 8, [pl], ["sp"])
        ext("m%d" % j, 32, ["M%d" % j], ["sm"])
        ts(part(T.WB, 128 * j - 128, 128), T.G16[:], cG, col(PL, 2), Op.is_equal, Op.mult, ["G16", "cF", pl], ["WB%d" % j], 128)
        ts(part(T.NT, 16 * j, 16), T.NT[:, 0:16], col(PL, 3), None, Op.add, None, ["NT0", pl], ["NT%d" % j])
        if j < 3:
            ts(part(T.WS, 144 * j, 144), XI[:], cG, col(PL, 2), Op.is_equal, Op.mult, ["XI", "cF", pl], ["WS%d" % j], 144)

    def hashes(src, bank, n, slot):
        tag = "u%d" % slot
        s = lambda k: part(T.UI, 16 * slot + 4 * k, n)
        cp(s(0), src, [bank], [tag + "s"])
        ts(s(1), s(0), 4095, None, Op.bitwise_and, None, [tag + "s"], [tag + "u"])
        tt(s(2), s(1), s(1), Op.mult, [tag + "u"], [tag + "sq"])
        cp(part(T.UF, 8 * slot, n), s(1), [tag + "u"], [tag + "uf"])
        ts(s(3), s(2), 5, 2047, Op.arith_shift_right, Op.bitwise_and, [tag + "sq"], [tag + "q"])
        cp(part(T.UF, 8 * slot + 4, n), s(3), [tag + "q"], [tag + "qf"])

    def xwin(t, h):
        if t == 0:
            return XO + 1024, ["X0"]
        return TC[t - 1] + 512 * (h + 1), ["X0"] + ["T%d%d%d" % (s, k, q) for s in range(t) for k in range(2) for q in range(2) if s < t - 1 or k <= h]

    def xb(t, h, since):
        k = 2 * t + h
        end, tok = xwin(since, h)
        for q in range(2):
            ts(T.XBO[:, 32 * k + q:32 * k + 32:2], T.ZE[:, 0:16], col(T.CB, 2 * h + q), float(aof(t, cq_of(h, q)) - XO),
               Op.add, Op.add, ["ZE", "CB%d" % h], ["XBO%d%d" % (k, q)])
        win = W[:, xs:A0 + end]
        rd = tok + ["XBO%d0" % k, "XBO%d1" % k]
        if since == 0 and not G1PE[k]:
            raw(part(T.XB, 512 * k, 512), win.indirect(part(T.XBO, 32 * k, 32)), rd, ["XB%da" % k, "XB%db" % k], 512)
            return
        raw(part(T.XB, 512 * k, 32), win.indirect(part(T.XBO, 32 * k, 2)), rd, ["XB%da" % k], 32)
        if G1PE[k]:
            mm([(ps[5][0:32, 128:256], part(T.XB, 512 * k, 32), T.ID[:], True, True)], 128, ["ID", "XB%da" % k], ["b5"])
            raw(T.XT[0:32, 128 * k:128 * k + 128], ps[5][0:32, 128:256], [], ["XT%d" % k, "b5"], 128, "v")
        else:
            raw(part(T.XB, 512 * k + 32, 480), win.indirect(part(T.XBO, 32 * k + 2, 30)), rd, ["XB%db" % k], 480)

    def offsets(t, h, slot, cols):
        k, tag, y = 2 * t + h, "u%d" % slot, 128 * h
        for q in range(2):
            ts(T.Y[:, y + q:y + 128:2], T.KK[:], col(T.UF, 8 * slot + cols[q]), col(T.UF, 8 * slot + 4 + cols[q]), Op.mult, Op.add,
               ["KK0", "KK1", tag + "uf", tag + "qf"], ["Y%d%d" % (h, q)])
        ry = ["Y%d0" % h, "Y%d1" % h]
        pp, lp, p2, l17 = part(T.PP, 64 * h, 64), part(T.LP, 64 * k, 64), part(T.P2, 64 * h, 64), part(T.L17, 64 * h, 64)
        ts(pp, part(T.Y, y, 64), 2047, None, Op.bitwise_and, None, ry, ["PP%d" % h])
        cp(part(T.PU, 64 * k, 64), pp, ["PP%d" % h], ["PU%d" % k])
        ts(lp, part(T.Y, y + 64, 64), 17, 7, Op.arith_shift_right, Op.bitwise_and, ry, ["LP%d" % k])
        tt(p2, pp, lp, Op.add, ["PP%d" % h, "LP%d" % k], ["P2%d" % h], 128)
        ts(part(T.P2U, 64 * k, 64), p2, 3.0, None, Op.add, None, ["P2%d" % h], ["P2U%d" % k])
        ts(l17, part(T.Y, y + 64, 64), 7 << 17, None, Op.bitwise_and, None, ry, ["L17%d" % h])
        tt(part(T.S0, 64 * k, 64), l17, pp, Op.add, ["PP%d" % h, "L17%d" % h], ["S0%d" % k], 128)

    def late(t, h, since, slot):
        k = 2 * t + h
        xb(t, h, since)
        mm([(ps[5][:, 0:2], sel(T.WS, 0, f), T.XB[:, 512 * k + f:512 * k + 32:16], f == 0, f == 15) for f in range(16)], 1024,
           ["WS0", "XB%da" % k], ["b5"])
        hashes(ps[5][:, 0:2], "b5", 2, slot)
        offsets(t, h, slot, (0, 1))

    def on_pe(out, tk, h, i, left, pattern, rl, src, rs):
        gc, bk, bn = part(T.GC, 1024 * h + 512 * i, 512), ps[6 + i], "b%d" % (6 + i)
        mm([(bk[:], left, pattern, True, False)], 512, rl, [bn])
        raw(gc, src, rs, ["GC%d%d" % (h, i)], 512)
        mm([(bk[:], T.ID[:], gc, False, True)], 512, ["ID", "GC%d%d" % (h, i)], [bn])
        mag(out, bk[:], [], [bn, tk])

    def distance(D, dn, t, h, off, on, bank, bn):
        k = 2 * t + h
        for i in range(2):
            o, tk = part(D, 1024 * h + 512 * i, 512), "%s%d%d" % (dn, h, i)
            src, rs = part(W, A0, XO).indirect(part(off, 64 * k + 32 * i, 32)), ["A", "Aw", "%s%d" % (on, k)]
            if dn == "DA" and G1PE[k]:
                on_pe(o, tk, h, i, T.XT[0:32, 128 * k:128 * k + 128], T.SM[0:32, :], ["SM", "XT%d" % k], src, rs)
                continue
            if dn == "DA":
                tt(o, src, part(T.XB, 512 * k, 512), Op.subtract, rs + ["XB%da" % k, "XB%db" % k], [tk], 512, "g")
            else:
                tt(o, src, part(T.XE, 1024 * h + 512 * i, 512), Op.subtract, rs + ["XE%d%d" % (h, i)], [tk], 512, "g")
            mag(o, o, [tk], [tk])
        out = bank[:, 0:64]
        mm([(out, T.BOs[:], T.RT[:], True, False), (out, T.BOs[:], T.RC[:], False, False)], 128, ["BOs", "RT", "RC"], [bn])
        mm([(out, sel(T.OS, 0, f), D[:, 1024 * h + f:1024 * h + 1024:16], False, f == 15) for f in range(16)], 1024,
           ["OS", "%s%d0" % (dn, h), "%s%d1" % (dn, h)], [bn])

    def pointers(h):
        for q in range(2):
            scale(part(T.E2, 32 * h + 16 * q, 16), T.MK[:], col(T.CB, 2 * h + q), ["MK", "CB%d" % h], ["E2%d%d" % (h, q)])
        mm([(part(ps[4], 32 * h, 32), T.BOf[:], part(T.E2, 32 * h, 32), True, True)], 256, ["BOf", "E2%d0" % h, "E2%d1" % h], ["b4"])

    def flanks(t, h):
        k = 2 * t + h
        bA, bB, nA, nB = banks(h)
        end, tok = xwin(t, h)
        for q in range(2):
            ts(T.XU[:, 64 * h + q:64 * h + 64:2], T.LP[:, 64 * k + q:64 * k + 64:2], col(T.CB, 2 * h + q), float(aof(t, cq_of(h, q)) + 3 - XO),
               Op.add, Op.add, ["LP%d" % k, "CB%d" % h], ["XU%d%d" % (h, q)])
        for i in range(2):
            raw(part(T.XE, 1024 * h + 512 * i, 512), W[:, xs:A0 + end].indirect(part(T.XU, 64 * h + 32 * i, 32)),
                tok + ["XU%d0" % h, "XU%d1" % h], ["XE%d%d" % (h, i)], 512)
        distance(T.DA, "DA", t, h, T.PU, "PU", bA, nA)
        s1, s2 = part(T.S1, 128 * h, 64), 128 * h + 64
        tt(s1, bA[:, 0:64], part(T.S0, 64 * k, 64), Op.min, [nA, "S0%d" % k], ["s1%d" % h])
        distance(T.DB, "DB", t, h, T.P2U, "P2U", bB, nB)
        tt(part(T.S1, s2, 64), bB[:, 0:64], s1, Op.min, [nB, "s1%d" % h], ["s2%d" % h])
        for q in range(2):
            o = 64 * h + 32 * q
            scan(part(T.SC, o, 32), T.C2K[:], T.S1[:, s2 + q:s2 + 64:2], -float(2 ** 22), Op.add, Op.max, ["s2%d" % h, "C2K"], ["SC%d%d" % (h, q)], 64)
            scale(part(T.E, 32 * h + 16 * q, 16), T.MK[:], col(T.SC, o + 31), ["MK", "SC%d%d" % (h, q)], ["E%d%d" % (h, q)])
        mm([(bA[:, 0:32], T.BOf[:], part(T.E, 32 * h, 32), True, True)], 256, ["BOf", "E%d0" % h, "E%d1" % h], [nA])
        a = aof(t, h)
        x0, x1, xm = part(T.XX, 64 * h, 32), part(T.XX, 64 * h + 32, 32), part(T.XM, 32 * h, 32)
        tt(x0, bA[:, 0:32], part(T.J, 16 * (3 * (a & 1) + (a >> 1)), 32), Op.add, [nA, "J"], ["x0%d" % h])
        ts(x1, x0, (1 << 23) | 2047, None, Op.bitwise_and, None, ["x0%d" % h], ["x1%d" % h])
        tt(xm, part(ps[4], 32 * h, 32), x1, Op.min, ["x1%d" % h, "b4"], ["xm%d" % h])
        ts(part(T.TU, 32 * h, 32), xm, cF, None, Op.add, None, ["xm%d" % h, "cF"], ["tu%d" % h])
        for q in range(2):
            tr, tk = part(W, A0 + TC[t] + 512 * h + 256 * q, 256), "T%d%d%d" % (t, h, q)
            raw(tr, W[:, A0:A0 + end].indirect(part(T.TU, 32 * h + 16 * q, 16)), tok + ["A", "Aw", "tu%d" % h], [tk], 256)
            scan(part(T.Z, 512 * h + 256 * q, 256), T.RS[:], tr, 0.0, Op.mult, Op.max, ["RS", tk], ["Z%d%d" % (h, q)], 128)

    def judge(t, h):
        j = t + 1
        bA, bB, nA, nB = banks(h)
        PL, zs, zt = T["PL%d" % j], T.Z[:, 512 * h + 15:512 * h + 512:16], ["Z%d0" % h, "Z%d1" % h]
        mm([(bB[:, 0:32], part(T.WB, 128 * t, 128), zs, True, True)], 64, ["WB%d" % j] + zt, [nB])
        mm([(bA[0:32, 0:128], zs, T.ID[:], True, True)], 128, ["ID"] + zt, [nA])
        raw(T.ZT[0:32, 128 * h:128 * h + 128], bA[0:32, 0:128], [], ["ZT%d" % h, nA], 128, "v")
        v = lambda i: part(T.VI, 192 * h + 32 * i, 32)
        tg = lambda s: "v%d%s" % (h, s)
        for q in range(2):
            cp(T.VI[:, 192 * h + q:192 * h + 32:2], part(bB, 16 * q, 16), [nB], [tg("s%d" % q)])
        ts(v(1), v(0), 4095, None, Op.bitwise_and, None, [tg("s0"), tg("s1")], [tg("u")])
        tt(v(2), v(1), v(1), Op.mult, [tg("u")], [tg("sq")])
        for b in range(2):
            ts(v(4 + b), v(1), col(PL, b), None, Op.mult, None, [tg("u"), "PL%d" % j], [tg("k%d" % b)])
        ts(v(3), v(2), 5, None, Op.arith_shift_right, None, [tg("sq")], [tg("q")])
        y = 128 * h
        for b in range(2):
            tt(T.YV[:, y + b:y + 64:2], v(4 + b), v(3), Op.add, [tg("q"), tg("k%d" % b)], ["YV%d%d" % (h, b)])
        ts(part(T.YV, y + 64, 64), part(T.YV, y, 64), 2047, None, Op.bitwise_and, None, ["YV%d0" % h, "YV%d1" % h], ["YW%d" % h])
        cp(part(T.MU, 64 * h, 64), part(T.YV, y + 64, 64), ["YW%d" % h], ["MU%d" % h])

    def message(t):
        ZM, zt = T["ZM%d" % t], ["Z00", "Z01", "Z10", "Z11"]
        raw(ZM[:, 0:64], T.Z[:, 15:1024:16], zt, ["ZM%d0" % t], 64, "v")
        mm([(ps[5][:, 4:8], sel(T.WS, 144 * (t + 1), f), T.Z[:, 16 * f + 15:1024:256], f == 0, f == 15) for f in range(16)], 1024,
           ["WS%d" % (t + 1)] + zt, ["b5"])
        cp(T.VC[:, 0:4], ps[5][:, 4:8], ["b5"], ["v4"])
        ts(T.VC[:, 4:8], T.VC[:, 0:4], 31, None, Op.bitwise_and, None, ["v4"], ["v5"])
        ts(T.VC[:, 8:12], T.VC[:, 4:8], 64.0, c4, Op.mult, Op.add, ["v5", "c4"], ["v6"])
        tt(ZM[:, 64:68], T.VC[:, 8:12], C[:, 24:28], Op.add, ["v6", "cq"], ["ZM%d1" % t])
        send(["ZM%d0" % t, "ZM%d1" % t], ["zs%d" % t], "z%d" % t)

    def verdict(t, h):
        j = t + 1
        bA, bB, nA, nB = banks(h)
        r, nw, cb = lambda q: col(T.RR, 4 * h + q), part(T.RR, 4 * h + 2, 2), part(T.CB, 2 * h, 2)
        for i in range(2):
            on_pe(part(T.DC, 1024 * h + 512 * i, 512), "DC%d%d" % (h, i), h, i, T.ZT[0:32, 128 * h:128 * h + 128], T.SL[0:32, 512 * i:512 * i + 512],
                  ["SL", "ZT%d" % h], T["M%d" % j][:, 0:2048].indirect(part(T.MU, 64 * h + 32 * i, 32)), ["M%d" % j, "MU%d" % h])
            mm([(bA[:, 0:64], sel(T.OS, 0, f), part(T.DC, 1024 * h + 64 * f, 64), f == 0, f == 15) for f in range(8 * i, 8 * i + 8)],
               512, ["OS", "DC%d%d" % (h, i)], [nA])
        for q in range(2):
            add(("dve",), ("v", 64), [nA], ["r%d%d" % (h, q)],
                lambda g, e, q=q: g.vector.tensor_reduce(r(q), part(bA, 32 * q, 32), AxisListType.X, Op.max))
        if t == 2:
            tt(nw, part(T.TCC, 8 + 2 * h, 2), cb, Op.subtract, ["cTc", "CB%d" % h], ["nw%d0" % h, "nw%d1" % h])
            mm([(bB[:, 0:32], T.BOf[:], part(T.E2, 32 * h, 32), True, False)], 256, ["BOf", "E2%d0" % h, "E2%d1" % h], [nB])
            for q in range(2):
                ts(part(T.E, 32 * h + 16 * q, 16), T.NT[:, 48:64], r(q), r(2 + q), Op.is_ge, Op.mult,
                   ["NT3", "r%d%d" % (h, q), "nw%d%d" % (h, q)], ["E%d%d" % (h, q)])
            mm([(bB[:, 0:32], T.BOf[:], part(T.E, 32 * h, 32), False, True)], 256, ["BOf", "E%d0" % h, "E%d1" % h], [nB])
            for q in range(2):
                ts(T.FU[:, cq_of(h, q):64:4], part(bB, 16 * q, 16), cF, None, Op.add, None, [nB, "cF"], ["FU%d" % (2 * h + q)])
            return
        for q in range(2):
            ts(r(2 + q), r(q), col(T["PL%d" % j], 3), col(T.TCC, 4 * t + 2 * h + q), Op.is_le, Op.mult,
               ["r%d%d" % (h, q), "PL%d" % j, "cTc"], ["nw%d%d" % (h, q)])
        if h == t:
            mm([(ps[5][:, 16:32], T.BOs[:], T.RA[:], True, False)], 64, ["BOs", "RA"], ["b5"])
            ts(T.E3[:], part(T.NT, 16 * j, 16), r(0), float(TC[t]), Op.is_ge, Op.mult, ["NT%d" % j, "r%d0" % h], ["E3"])
            mm([(ps[5][:, 16:32], T.BOs[:], T.E3[:], False, True)], 64, ["BOs", "E3"], ["b5"])
            ts(T.AU[:], ps[5][:, 16:32], 1.0 / BIG, col(C, 12 + t), Op.mult, Op.add, ["b5", "cFT"], ["AU"])
            cp(W[:, A0 - TC[t]:A0 + 1024].indirect(T.AU[:]), part(W, A0 + TC[t] + 512 * h, 256), ["AU", "T%d%d0" % (t, h)], ["A"], 256, "sc")
            if t == 0:
                raw(part(W, A0 + 2048, 16), part(W, A0, 16), ["A"], ["Aw"], 64, "v")
        tt(cb, cb, nw, Op.max, ["nw%d0" % h, "nw%d1" % h, "CB%d" % h], ["CB%d" % h])
        pointers(h)

    def update(i, j, t):
        ZL = T["ZL%d" % i]
        ext("z%d" % i, 4, ["ZL%d" % i], ["zs%d" % t])
        cp(part(T.ZU, 4 * i, 4), ZL[:, 64:68], ["ZL%d" % i], ["ZU%d" % i])
        cp(T["M%d" % j][:, 0:2048].indirect(part(T.ZU, 4 * i, 4)), ZL[:, 0:64], ["ZU%d" % i, "ZL%d" % i], ["M%d" % j], 64, "sc")

    mm([(ps[6][:, 0:4], sel(T.WS, 0, f), W[:, xs + 64 * f:xs + 64 * f + 52:17], f == 0, f == 15) for f in range(16)], 1024, ["WS0", "X0"], ["b6"])
    hashes(ps[6][:, 0:4], "b6", 4, 0)
    for h in range(2):
        xb(0, h, 0)
        offsets(0, h, 0, (h, h + 2))
        pointers(h)
    mm([(ps[7][:, 0:2], sel(T.WS, 0, f), W[:, xs + 64 * f + 16:xs + 64 * f + 51:34], f == 0, f == 15) for f in range(16)], 1024, ["WS0", "X0"], ["b7"])
    hashes(ps[7][:, 0:2], "b7", 2, 1)
    xb(1, 1, 0)
    offsets(1, 1, 1, (0, 1))
    for t in range(3):
        hs = (t & 1, 1 - (t & 1))
        for h in hs:
            flanks(t, h)
        for h in hs:
            judge(t, h)
        if t < 2:
            message(t)
        if t == 1:
            update(0, 2, 0)
        if t == 2:
            update(1, 3, 0)
            update(2, 3, 1)
        verdict(t, hs[0])
        if t == 0:
            late(1, 0, 1, 2)
            late(2, 0, 1, 3)
        if t == 1:
            late(2, 1, 2, 4)
        verdict(t, hs[1])
    tok = xwin(3, 1)[1] + ["A", "Aw"] + ["FU%d" % c for c in range(4)]
    for i, e in enumerate(("dve", "act")):
        raw(part(T.YO, 512 * i, 512), part(W, A0, 6176).indirect(part(T.FU, 32 * i, 32)), tok, ["YO%d" % i], 512, "g", (e,))
        dma("sync" if i == 0 else "act", part(T.y, 512 * i, 512), part(T.YO, 512 * i, 512), "sy%d" % i, ["y%d" % i], ["YO%d" % i])
    return ops


def _deps(ops):
    last, readers, deps, soft = {}, {}, [], []
    for i, o in enumerate(ops):
        d, s = set(last[t] for t in o["r"] if t in last), set()
        for t in o["w"]:
            order_only = t in ("q0", "q1", "gq")
            if t in last:
                (s if order_only else d).add(last[t])
            d.update(readers.get(t, ()))
        d.discard(i)
        deps.append(sorted(d))
        soft.append(sorted(s - d))
        for t in o["r"]:
            readers.setdefault(t, []).append(i)
        for t in o["w"]:
            last[t] = i
            readers[t] = []
    return deps, soft


def _cost(o, e, P):
    k, n = o["cost"]
    c = P["cyc"]
    if k == "v":
        x = max(64, n) * c + (15 if e == "act" else 0)
    elif k == "g":
        x = (65 if e == "act" else 50) + n * c * P["gam"]
    elif k == "sc":
        x = 50 + n * c * P["sc"]
    elif k == "p":
        x = n * P["pe"]
    elif k == "i":
        x = 130 + 2 * n * c
    elif k == "s":
        x = 400.0
    elif k == "d":
        return 60.0, (2000.0 if n in ("sy0", "sy1") else P.get(n, P["lsmall"]))
    else:
        return 0.0, (P["zlat"] if n[0] == "z" else P[n])
    return x, x


def _replay(ops, deps, order, eng, P):
    free, done = {}, {}
    for i in order:
        e = eng[i]
        st = free.get(e, 0.0)
        for d in deps[i]:
            st = max(st, done[d] + (0.0 if e == "pe" and eng[d] == "pe" else P["sem"]))
        hold, lat = _cost(ops[i], e, P)
        if e != "ext":
            free[e] = st + hold
        done[i] = st + lat
    return done


def _schedule(ops, deps, soft, succ, P, prio, pen, slack):
    n = len(ops)
    free = {e: 0.0 for e in ("dve", "act", "pe", "pool", "sync", "ext")}
    done, eng, order, at = [0.0] * n, [None] * n, [], {}
    left = [len(deps[i]) + len(soft[i]) for i in range(n)]
    ready = [i for i in range(n) if left[i] == 0]
    while ready:
        best = []
        for i in ready:
            o = ops[i]
            if i not in at:
                at[i] = max([0.0] + [done[d] + (0.0 if o["eng"][0] == "pe" and eng[d] == "pe" else P["sem"]) for d in deps[i]])
            e = o["eng"][0]
            st = max(free[e], at[i])
            if len(o["eng"]) > 1 and max(free["dve"], at[i]) + pen[i] < st:
                e, st = "dve", max(free["dve"], at[i])
            best.append((st, i, e))
        m = min(b[0] for b in best)
        st, i, e = max([b for b in best if b[0] <= m + slack], key=lambda b: (prio[b[1]], -b[1]))
        hold, lat = _cost(ops[i], e, P)
        if e != "ext":
            free[e] = st + hold
        done[i], eng[i] = st + lat, e
        order.append(i)
        ready.remove(i)
        for s in succ[i]:
            left[s] -= 1
            if left[s] == 0:
                ready.append(s)
    return order, eng


def _plan(ops, deps, soft, steps):
    n = len(ops)
    succ = [[] for _ in range(n)]
    for i in range(n):
        for d in deps[i] + soft[i]:
            succ[d].append(i)
    models = [dict(EST, **v) for v in VARIANTS]
    x = [12345]

    def rnd():
        x[0] = (x[0] * 1103515245 + 12345) % 2147483648
        return x[0] / 2147483648.0
    prio = [0.0] * n
    for i in range(n - 1, -1, -1):
        prio[i] = _cost(ops[i], ops[i]["eng"][0], EST)[1] + EST["sem"] + max([prio[s] for s in succ[i]], default=0.0)
    pen, slack, best = [800.0] * n, 120.0, None
    for step in range(steps + 1):
        p2, q2, s2 = list(prio), list(pen), slack
        if step:
            share, amp = 0.01 + 0.12 * rnd(), 100.0 + 1500.0 * rnd()
            for i in range(n):
                if rnd() < share:
                    p2[i] += amp * (2 * rnd() - 1)
                if rnd() < share:
                    q2[i] = 2500.0 * rnd() * rnd()
            if rnd() < 0.2:
                s2 = 30.0 + 300.0 * rnd()
        order, eng = _schedule(ops, deps, soft, succ, EST, p2, q2, s2)
        val = sum(max(_replay(ops, deps, order, eng, P).values()) for P in models) / len(models)
        if best is None or val <= best[0]:
            best, prio, pen, slack = (val, order, eng), p2, q2, s2
    return best


_PLAN = {}


def _emit(g, T, ops):
    deps, soft = _deps(ops)
    if "p" not in _PLAN:
        _PLAN["p"] = _plan(ops, deps, soft, STEPS)
    _v, order, eng = _PLAN["p"]
    place = {i: k for k, i in enumerate(order)}
    queue = {"dve": g.vector, "act": g.scalar, "pe": g.tensor, "pool": g, "sync": g.sync}
    silent = lambda d, i: eng[d] == "pe" and eng[i] == "pe"
    need = set(d for i in range(len(ops)) if eng[i] != "ext" for d in deps[i] if not silent(d, i))
    count = {e: 0 for e in queue}
    mark, seen, total = {}, {}, {}
    known = {e: {} for e in queue}
    for i in order:
        o, e = ops[i], eng[i]
        if e == "ext":
            mark[i], seen[i] = o["sem"], {}
            total[o["sem"][0]] = o["sem"][1]
            continue
        kn = known[e]
        for d in sorted(deps[i], key=lambda d: -place[d]):
            if silent(d, i):
                continue
            s, v = mark[d]
            if kn.get(s, 0) < v:
                queue[e].wait_ge(T.sem[s], v)
                kn[s] = v
                for s2, v2 in seen[d].items():
                    kn[s2] = max(kn.get(s2, 0), v2)
        ins = o["fn"](g, e)
        seen[i] = dict(kn)
        if o["sem"]:
            ins.then_inc(T.sem[o["sem"][0]], 16)
            mark[i] = o["sem"]
            total[o["sem"][0]] = 16
        elif i in need:
            count[e] += 1
            ins.then_inc(T.sem[e], 1)
            mark[i] = (e, count[e])
            total[e] = count[e]
    return total


def _bits(engines):
    return sum(1 << e for e in engines)


def _ports(core, T, topo):
    c = [p for p in topo.cores_of(core) if p != core and all(topo.may_write(p, d) for d in T.cores)]
    own = [p for p in c if topo.die(p) == topo.die(core)]
    far = [p for p in c if topo.die(p) != topo.die(core)]
    return [own[0], far[0], own[1], far[1]]


def _z_targets(q, t, T):
    n = len(T.cores)
    if t == 0:
        return [(T.cores[(q - 1) % n], "ZL0", "z0"), (T.cores[(q - 2) % n], "ZL1", "z1")]
    return [(T.cores[(q - 1) % n], "ZL2", "z2")]


def _fused(g, T, topo, core, items, width):
    tr = []
    for k, (d, src, dst, sem) in enumerate(items):
        rid, pid = topo.addr(d, core)
        tr.append(RemoteDMATransfer(dst_ids=[DstId(rid=rid, pnc=pid)], dma_engine_mask=_bits(topo.engines(core, d)[k * width:(k + 1) * width]),
                                    remote_sem=T.sem[sem], src=src, dst=dst))
    g.remote_dma_fused(tr, local_sem=T.sem.sent)
    return width * len(items)


def _rank(g, core, T, topo, rank):
    ports = _ports(core, T, topo)
    sent = [0]

    def par(g, e):
        ids = [DstId(rid=topo.addr(p, core)[0], pnc=topo.addr(p, core)[1]) for p in ports[:3]]
        g.remote_dma_fused([RemoteDMATransfer(dst_ids=ids, dma_engine_mask=topo.mask(core, ports[0]), remote_sem=T.sem.rpar,
                                              src=T.PM[:], dsts=[T.PR[:]] * 3)], local_sem=T.sem.sent)
        sent[0] += len(topo.engines(core, ports[0]))

    def mem(i):
        def fn(g, e):
            sent[0] += _fused(g, T, topo, core, [(ports[k], T.MO[:, 512 * k:512 * k + 512], T.RB[:], "rq") for k in (2 * i, 2 * i + 1)], 8)
        return fn

    def zs(t):
        def fn(g, e):
            tg = _z_targets(rank, t, T)
            items = [(d, T["ZM%d" % t][:], T[b][:], s) for d, b, s in tg if topo.may_write(core, d)]
            if len(items) < len(tg):
                items.append((ports[2], T["ZM%d" % t][:], T["ZR%d" % t][:], "rz%d" % t))
            sent[0] += _fused(g, T, topo, core, items, 4)
        return fn
    total = _emit(g, T, _build(T, {"par": par, "m0": mem(0), "m1": mem(1), "z0": zs(0), "z1": zs(1)}))
    g.wait_ge(T.sem.sent, sent[0])
    for s in sorted(total):
        g.wait_ge(T.sem[s], total[s])


def _relay(g, core, T, topo, rank, k):
    n, home = len(T.cores), T.cores[rank]
    sent = [0]

    def hand(d, src, dst, sem):
        sent[0] += _fused(g, T, topo, core, [(d, src, dst, sem)], 8)

    def zs(t):
        items = [(d, T["ZR%d" % t][:], T[b][:], s) for d, b, s in _z_targets(rank, t, T) if not topo.may_write(home, d)]
        if k == 2 and items:
            g.wait_ge(T.sem["rz%d" % t], 4)
            sent[0] += _fused(g, T, topo, core, items, 4)
    if k < 3:
        g.wait_ge(T.sem.rpar, len(topo.engines(home, core)))
        hand(T.cores[(rank - k - 1) % n], T.PR[:], T["PL%d" % (k + 1)][:], "par%d" % (k + 1))
    g.wait_ge(T.sem.rq, 8)
    for j in (1, 2, 3):
        if j == 3:
            zs(0)
        hand(T.cores[(rank - j) % n], T.RB[:], T["M%d" % j][:, 512 * k:512 * k + 512], "m%d" % j)
    zs(1)
    g.wait_ge(T.sem.sent, sent[0])


def rank_program(g, core, T, topo):
    rank = T.rank_of(core)
    if rank is not None:
        _rank(g, core, T, topo, rank)
        return
    for r, c in enumerate(T.cores):
        if core in topo.cores_of(c) and core in _ports(c, T, topo):
            _relay(g, core, T, topo, r, _ports(c, T, topo).index(core))
